import numpy as np
import ml_dtypes


def mxq(x, axis, fmt="e4m3"):
    dtype, down = {"e4m3": (ml_dtypes.float8_e4m3fn, 7), "e5m2": (ml_dtypes.float8_e5m2, 14)}[fmt]
    v = np.moveaxis(np.asarray(x, np.float32).astype(ml_dtypes.bfloat16).astype(np.float64), axis, -1)
    blocks = v.reshape(v.shape[:-1] + (-1, 32))
    amax = np.abs(blocks).max(-1, keepdims=True)
    byte = np.maximum(np.where(amax > 0, np.frexp(amax)[1] - 1 + 127, 0) - down, 1)
    scale = np.exp2(byte - 127.0)
    codes = (blocks / scale).astype(np.float32).astype(dtype).astype(np.float64)
    return np.moveaxis((codes * scale).reshape(v.shape), -1, axis)


WIDE = False


def mx_kscale(k):
    if not WIDE:
        return np.ones(k)
    levels = np.array([10, -10, 5, -5, 0])
    if k % 512:
        return np.exp2(np.random.permutation(np.resize(levels, k // 32))).repeat(32)
    a = np.empty((k // 512, 16))
    for p in range(k // 512):
        a[p, :8] = np.random.permutation(np.resize(levels, 8))
        for g in range(8):
            far = levels[np.abs(levels - a[p, g]) >= 10]
            a[p, g + 8] = far[np.random.randint(len(far))]
    return np.exp2(a.ravel()).repeat(32)


def f64(x):
    return np.asarray(x).astype(np.float64)


def striped(idx):
    return np.tile(idx.reshape(-1, 16).T, (8, 1)).astype(np.uint16)


def unstriped(offs):
    return offs[:16].T.reshape(-1).astype(np.int64)


E2M1 = np.array([0.0, 0.5, 1.0, 1.5, 2.0, 3.0, 4.0, 6.0, -0.0, -0.5, -1.0, -1.5, -2.0, -3.0, -4.0, -6.0])


def pack_weight(w, fmt):
    k, n = w.shape
    w = f64(np.asarray(w, np.float32).astype(ml_dtypes.bfloat16)).reshape(k // 32, 32, n)
    amax = np.abs(w).max(1)
    if fmt == "e4m3":
        byte = np.frexp(amax)[1] - 1 + 127 - 7
    else:
        mant, ex = np.frexp(amax / 6.0)
        byte = np.where(mant > 0.5, ex, ex - 1) + 127
    byte = np.clip(np.where(amax > 0, byte, 1), 1, 254)
    scaled = (w * np.exp2(127.0 - byte)[:, None, :]).reshape(k, n).astype(np.float32)
    by_word = np.ascontiguousarray(scaled.reshape(k // 512, 128, 4, n).transpose(0, 1, 3, 2))
    if fmt == "e4m3":
        words = by_word.astype(ml_dtypes.float8_e4m3fn).view(np.uint8)
    else:
        c = by_word.astype(ml_dtypes.float4_e2m1fn).view(np.uint8) & 0xF
        words = (c[..., 0::2] | (c[..., 1::2] << 4)).reshape(k // 512, 128, 2 * n)
    return np.ascontiguousarray(words), np.ascontiguousarray(byte.astype(np.uint8).reshape(k // 512, 16, n))


def unpack_weight(words, scales, fmt):
    g, _, n = scales.shape
    words = np.ascontiguousarray(words).reshape(g, 128, n, -1)
    if fmt == "e4m3":
        vals = words.view(ml_dtypes.float8_e4m3fn).astype(np.float64)
    else:
        nib = np.empty((g, 128, n, 4), np.uint8)
        nib[..., 0::2] = words & 0xF
        nib[..., 1::2] = words >> 4
        vals = E2M1[nib]
    vals = vals * np.repeat(np.exp2(scales.astype(np.float64) - 127.0), 8, axis=1)[..., None]
    return vals.transpose(0, 1, 3, 2).reshape(g * 512, n)


def silu(v):
    return v / (1.0 + np.exp(-np.maximum(v, -700.0)))


K, T, E, C, H, N = 1024, 1024, 2, 256, 1024, 256


def by_expert(wq, xq):
    return np.concatenate([wq[e].T @ xq[:, e * C:(e + 1) * C] for e in range(E)], axis=1)


def setup_inputs():
    n = np.random.standard_normal
    s = mx_kscale(K)[:, None]
    u = mx_kscale(H)
    w1 = [pack_weight(m, "e2m1") for m in n((E, K, H)) / np.sqrt(K) / s[None]]
    w3 = [pack_weight(m, "e2m1") for m in n((E, K, H)) / np.sqrt(K) / s[None] * u[None, None, :]]
    w2 = [pack_weight(m, "e2m1") for m in n((E, H, N)) / np.sqrt(H) / u[None, :, None]]
    x = pack_weight(n((K, T)) * s, "e4m3")
    return {
        "x_words": x[0],
        "x_scales": x[1],
        "xr": n((N, T)).astype(np.float32),
        "w1_words": np.stack([m[0] for m in w1]),
        "w1_scales": np.stack([m[1] for m in w1]),
        "w3_words": np.stack([m[0] for m in w3]),
        "w3_scales": np.stack([m[1] for m in w3]),
        "w2_words": np.stack([m[0] for m in w2]),
        "w2_scales": np.stack([m[1] for m in w2]),
        "gate": np.tile(np.random.uniform(0.2, 1.0, E * C), (N, 1)).astype(np.float32),
        "offs": striped(np.random.permutation(T)[:E * C]),
    }


def reference(x_words, x_scales, xr, w1_words, w1_scales, w3_words, w3_scales, w2_words, w2_scales, gate, offs):
    idx = unstriped(offs)
    w1 = np.stack([unpack_weight(w1_words[e], w1_scales[e], "e2m1") for e in range(E)])
    w3 = np.stack([unpack_weight(w3_words[e], w3_scales[e], "e2m1") for e in range(E)])
    w2 = np.stack([unpack_weight(w2_words[e], w2_scales[e], "e2m1") for e in range(E)])
    xq = unpack_weight(x_words, x_scales, "e4m3")[:, idx]
    h = silu(by_expert(w1, xq))
    h = h * by_expert(w3, xq)
    y = by_expert(w2, mxq(h, 0, "e4m3"))
    out = f64(xr).copy()
    out[:, idx] += f64(gate) * y
    return out

@@ -1,0 +1,223 @@
+from contextlib import ExitStack
+
+import concourse.mybir as mybir
+from concourse.masks import make_identity
+
+K, T, E, C, H, N = 1024, 1024, 2, 256, 1024, 256
+FLOPS = 2 * E * C * (2 * K * H + H * N)
+
+F32 = mybir.dt.float32
+BF16 = mybir.dt.bfloat16
+I32 = mybir.dt.int32
+U32 = mybir.dt.uint32
+U16 = mybir.dt.uint16
+U8 = mybir.dt.uint8
+FP8X4 = mybir.dt.float8_e4m3fn_x4
+FP4X4 = mybir.dt.float4_e2m1fn_x4
+MULT = mybir.AluOpType.mult
+ADD = mybir.AluOpType.add
+SILU = mybir.ActivationFunctionType.Silu
+
+P = 128
+PASS = 512
+KP = K // PASS
+HP = H // PASS
+SLOTS = E * C
+BLOCKS = SLOTS // P
+NB = N // P
+
+
+def tile_moe_res_glu_silu_kernel(tc, x_words, x_scales, xr, w1_words, w1_scales, w3_words, w3_scales, w2_words, w2_scales, gate, offs, out):
+    nc = tc.nc
+    with ExitStack() as ctx:
+        keep = ctx.enter_context(tc.tile_pool(name="keep", bufs=1))
+        ring = ctx.enter_context(tc.tile_pool(name="ring", bufs=3))
+        psum = ctx.enter_context(tc.psum_pool(name="psum", bufs=1))
+
+        offsets = keep.tile([P, SLOTS // 16], U16, name="offsets")
+        nc.sync.dma_start(offsets[:], offs)
+
+        def load_planes(name, scales, planes, width, queue):
+            tile = keep.tile([P, planes * width], U8, name=name, align_bytes=64)
+            words = tile[:].bitcast(I32)
+            nc.vector.memset(words, 0)
+            rows = scales.bitcast(I32).rearrange("g (q r) w -> r q g w", r=4)
+            for r in range(4):
+                queue.dma_start(words[r:P:32, :].rearrange("q (g w) -> q g w", g=planes), rows[r])
+            return tile
+
+        def load_words(name, words_hbm):
+            tile = keep.tile([P, words_hbm.shape[1]], U8, name=name, align_bytes=64)
+            nc.sync.dma_start(tile[:].bitcast(I32), words_hbm.bitcast(I32))
+            return tile
+
+        def load_tokens(o):
+            tile = keep.tile([P, T], I32, name="xw%d" % o, align_bytes=64)
+            nc.sync.dma_start(tile[:], x_words[o].rearrange("p t r -> p (t r)").bitcast(I32))
+            return tile
+
+        zero = keep.tile([P, 2], F32, name="zero")
+        nc.gpsimd.memset(zero[:, 0:1], 0.0)
+        nc.scalar.activation(zero[:, 1:2], zero[:, 0:1], SILU)
+
+        def load_half(name, words_hbm, hf):
+            tile = keep.tile([P, KP * 2 * PASS], U8, name=name, align_bytes=64)
+            nc.sync.dma_start(tile[:].bitcast(I32).rearrange("p (s w) -> p s w", s=KP),
+                              words_hbm[:, :, hf * 2 * PASS:(hf + 1) * 2 * PASS].bitcast(I32).rearrange("s p w -> p s w"))
+            return tile
+
+        xw = {}
+        wv = {}
+        ws = {}
+        xw[0] = load_tokens(0)
+        xs = load_planes("xs", x_scales, KP, T, nc.sync)
+        t = load_words("w1w00", w1_words[0, 0])
+        for hf in range(HP):
+            wv[0, 0, 0, hf] = t[:, hf * 2 * PASS:(hf + 1) * 2 * PASS]
+        ws[0] = load_planes("w1s", w1_scales.rearrange("e s q i -> (e s) q i"), E * KP, H, nc.sync)
+        xw[1] = load_tokens(1)
+        t = load_words("w1w01", w1_words[0, 1])
+        for hf in range(HP):
+            wv[0, 0, 1, hf] = t[:, hf * 2 * PASS:(hf + 1) * 2 * PASS]
+        ws[1] = load_planes("w3s", w3_scales.rearrange("e s q i -> (e s) q i"), E * KP, H, nc.gpsimd)
+        for hf in range(HP):
+            t = load_half("w3w0%d" % hf, w3_words[0], hf)
+            for o in range(KP):
+                wv[1, 0, o, hf] = t[:, o * 2 * PASS:(o + 1) * 2 * PASS]
+
+        def load_both(name, m, words_hbm):
+            tile = keep.tile([P, KP * 2 * H], U8, name=name, align_bytes=64)
+            nc.sync.dma_start(tile[:].bitcast(I32).rearrange("p (s w) -> p s w", s=KP),
+                              words_hbm.bitcast(I32).rearrange("s p w -> p s w"))
+            for o in range(KP):
+                for hf in range(HP):
+                    c0 = (o * H + hf * PASS) * 2
+                    wv[m, 1, o, hf] = tile[:, c0:c0 + 2 * PASS]
+
+        load_both("w1w1", 0, w1_words[1])
+        w2s = load_planes("w2s", w2_scales.rearrange("e s q n -> (e s) q n"), E * HP, N, nc.gpsimd)
+        w2w = keep.tile([P, E * HP * 2 * N], U8, name="w2w", align_bytes=64)
+        nc.sync.dma_start(w2w[:].bitcast(I32).rearrange("p (g w) -> p g w", g=E * HP),
+                          w2_words.bitcast(I32).rearrange("e s p w -> p (e s) w"))
+        gates = keep.tile([P, SLOTS], F32, name="gates")
+        nc.sync.dma_start(gates[:], gate[0:P, :])
+        load_both("w3w1", 1, w3_words[1])
+        resid = []
+        for nb in range(NB):
+            tile = keep.tile([P, T], F32, name="resid%d" % nb)
+            nc.sync.dma_start(tile[:], xr[nb * P:(nb + 1) * P, :])
+            resid.append(tile)
+
+        ident = keep.tile([P, P], F32, name="ident")
+        make_identity(nc, ident[:])
+
+        spread = []
+        for nb in range(NB):
+            tile = keep.tile([P, T], F32, name="spread%d" % nb)
+            nc.scalar.copy(tile[:], zero[:, 0:1].to_broadcast([P, T]))
+            spread.append(tile)
+
+        gw = [keep.tile([P, SLOTS], U32, name="gw%d" % o, align_bytes=64) for o in range(KP)]
+        gs = [keep.tile([P, SLOTS], U8, name="gs%d" % o, align_bytes=64) for o in range(KP)]
+        for o in range(KP):
+            for lo, hi in ((0, P), (P, C), (C, SLOTS)):
+                lst = offsets[:, lo // 16:hi // 16]
+                nc.vector.tensor_copy(gw[o][:, lo:hi], xw[o][:].bitcast(U32).indirect(lst))
+                nc.vector.tensor_copy(gs[o][:, lo:hi], xs[:, o * T:(o + 1) * T].indirect(lst))
+
+        acts = {}
+        hid = {}
+        codes = {}
+        planes = {}
+
+        def product(m, units):
+            banks = [psum.tile([P, PASS], F32, name="ab", bufs=6) for unit in units]
+            for o in range(KP):
+                for bank, (b, hf) in zip(banks, units):
+                    e = b * P // C
+                    cols = slice(b * P, (b + 1) * P)
+                    s0 = (e * KP + o) * H + hf * PASS
+                    nc.tensor.matmul_mx(
+                        out=bank[:],
+                        lhsT=gw[o][:, cols].bitcast(FP8X4), lhsT_scale=gs[o][:, cols],
+                        rhs=wv[m, e, o, hf].bitcast(FP4X4), rhs_scale=ws[m][:, s0:s0 + PASS],
+                        start=(o == 0), stop=(o == KP - 1))
+            return banks
+
+        def gated(units):
+            for bank, unit in zip(product(0, units), units):
+                acts[unit] = ring.tile([P, PASS], F32, name="act", bufs=4)
+                nc.scalar.activation(acts[unit][:].rearrange("j (u p d) -> j u p d", u=2, d=2),
+                                     bank[:].rearrange("j (p u d) -> j u p d", u=2, d=2), SILU)
+
+        def hidden(unit):
+            bank = product(1, [unit])[0]
+            hid[unit] = ring.tile([P, PASS], BF16, name="h", bufs=4)
+            nc.vector.tensor_tensor(hid[unit][:].rearrange("j (u p d) -> j u p d", u=2, d=2),
+                                    bank[:].rearrange("j (p u d) -> j u p d", u=2, d=2),
+                                    acts[unit][:].rearrange("j (u p d) -> j u p d", u=2, d=2), MULT)
+
+        def turn(b, halves):
+            n = len(halves)
+            bank = psum.tile([P, n * 2 * P], F32, name="turned")
+            for i, hf in enumerate(halves):
+                pairs = hid[b, hf][:].bitcast(F32)
+                for u in range(2):
+                    nc.tensor.transpose(bank[:, (i * 2 + u) * P:(i * 2 + u + 1) * P], pairs[:, u * P:(u + 1) * P], ident[:])
+            ht = ring.tile([P, n * 2 * P], F32, name="ht", align_bytes=64)
+            nc.scalar.copy(ht[:].rearrange("p (s j u) -> p s j u", s=n, u=2),
+                           bank[:].rearrange("p (s u j) -> p s j u", s=n, u=2))
+            words = ring.tile([P, n * P], U32, name="hcodes", align_bytes=64)
+            scales = ring.tile([P, n * P], U8, name="hscales", align_bytes=64)
+            nc.vector.quantize_mx(out=words[:].bitcast(FP8X4), scales=scales[:], in_=ht[:].bitcast(BF16))
+            for i, hf in enumerate(halves):
+                codes[b, hf] = words[:, i * P:(i + 1) * P]
+                planes[b, hf] = scales[:, i * P:(i + 1) * P]
+
+        def second_layer(b):
+            e = b * P // C
+            bank = psum.tile([P, NB * P], F32, name="ybank")
+            for nb in range(NB):
+                for s in range(HP):
+                    g = e * HP + s
+                    nc.tensor.matmul_mx(
+                        out=bank[:, nb * P:(nb + 1) * P],
+                        lhsT=w2w[:, (g * N + nb * P) * 2:(g * N + (nb + 1) * P) * 2].bitcast(FP4X4),
+                        lhsT_scale=w2s[:, g * N + nb * P:g * N + (nb + 1) * P],
+                        rhs=codes[b, s].bitcast(FP8X4),
+                        rhs_scale=planes[b, s],
+                        start=(s == 0), stop=(s == HP - 1))
+            y = ring.tile([P, NB * P], F32, name="y")
+            nc.scalar.copy(y[:], bank[:])
+            lst = offsets[:, b * P // 16:(b + 1) * P // 16]
+            for nb in range(NB):
+                nc.vector.tensor_tensor(spread[nb][:].indirect(lst), y[:, nb * P:(nb + 1) * P], gates[:, b * P:(b + 1) * P], MULT)
+
+        gated([(0, 0), (0, 1), (1, 0), (1, 1)])
+        hidden((0, 0))
+        hidden((0, 1))
+        hidden((1, 0))
+        turn(0, (0, 1))
+        hidden((1, 1))
+        gated([(2, 0)])
+        second_layer(0)
+        turn(1, (0, 1))
+        gated([(2, 1)])
+        hidden((2, 0))
+        hidden((2, 1))
+        second_layer(1)
+        gated([(3, 0)])
+        gated([(3, 1)])
+        turn(2, (0, 1))
+        hidden((3, 0))
+        hidden((3, 1))
+        turn(3, (0,))
+        second_layer(2)
+        turn(3, (1,))
+        second_layer(3)
+
+        for nb in range(NB):
+            for c0 in range(0, T, PASS):
+                res = ring.tile([P, PASS], F32, name="res", bufs=4)
+                nc.vector.tensor_tensor(res[:], spread[nb][:, c0:c0 + PASS], resid[nb][:, c0:c0 + PASS], ADD)
+                nc.sync.dma_start(out[nb * P:(nb + 1) * P, c0:c0 + PASS], res[:])

@@ -37,13 +37,13 @@ def tile_moe_res_glu_silu_kernel(tc, x_words, x_scales, xr, w1_words, w1_scales,
         offsets = keep.tile([P, SLOTS // 16], U16, name="offsets")
         nc.sync.dma_start(offsets[:], offs)
 
-        def load_planes(name, scales, planes, width, queue):
+        def load_planes(name, scales, planes, width, clearer):
             tile = keep.tile([P, planes * width], U8, name=name, align_bytes=64)
             words = tile[:].bitcast(I32)
-            nc.vector.memset(words, 0)
+            clearer.memset(words, 0)
             rows = scales.bitcast(I32).rearrange("g (q r) w -> r q g w", r=4)
             for r in range(4):
-                queue.dma_start(words[r:P:32, :].rearrange("q (g w) -> q g w", g=planes), rows[r])
+                nc.sync.dma_start(words[r:P:32, :].rearrange("q (g w) -> q g w", g=planes), rows[r])
             return tile
 
         def load_words(name, words_hbm):
@@ -57,7 +57,7 @@ def tile_moe_res_glu_silu_kernel(tc, x_words, x_scales, xr, w1_words, w1_scales,
             return tile
 
         zero = keep.tile([P, 2], F32, name="zero")
-        nc.gpsimd.memset(zero[:, 0:1], 0.0)
+        nc.vector.memset(zero[:, 0:1], 0.0)
         nc.scalar.activation(zero[:, 1:2], zero[:, 0:1], SILU)
 
         def load_half(name, words_hbm, hf):
@@ -69,17 +69,17 @@ def tile_moe_res_glu_silu_kernel(tc, x_words, x_scales, xr, w1_words, w1_scales,
         xw = {}
         wv = {}
         ws = {}
+        xs = load_planes("xs", x_scales, KP, T, nc.gpsimd)
         xw[0] = load_tokens(0)
-        xs = load_planes("xs", x_scales, KP, T, nc.sync)
         t = load_words("w1w00", w1_words[0, 0])
         for hf in range(HP):
             wv[0, 0, 0, hf] = t[:, hf * 2 * PASS:(hf + 1) * 2 * PASS]
-        ws[0] = load_planes("w1s", w1_scales.rearrange("e s q i -> (e s) q i"), E * KP, H, nc.sync)
+        ws[0] = load_planes("w1s", w1_scales.rearrange("e s q i -> (e s) q i"), E * KP, H, nc.gpsimd)
         xw[1] = load_tokens(1)
         t = load_words("w1w01", w1_words[0, 1])
         for hf in range(HP):
             wv[0, 0, 1, hf] = t[:, hf * 2 * PASS:(hf + 1) * 2 * PASS]
-        ws[1] = load_planes("w3s", w3_scales.rearrange("e s q i -> (e s) q i"), E * KP, H, nc.gpsimd)
+        ws[1] = load_planes("w3s", w3_scales.rearrange("e s q i -> (e s) q i"), E * KP, H, nc.vector)
         for hf in range(HP):
             t = load_half("w3w0%d" % hf, w3_words[0], hf)
             for o in range(KP):
@@ -95,18 +95,15 @@ def tile_moe_res_glu_silu_kernel(tc, x_words, x_scales, xr, w1_words, w1_scales,
                     wv[m, 1, o, hf] = tile[:, c0:c0 + 2 * PASS]
 
         load_both("w1w1", 0, w1_words[1])
-        w2s = load_planes("w2s", w2_scales.rearrange("e s q n -> (e s) q n"), E * HP, N, nc.gpsimd)
+        load_both("w3w1", 1, w3_words[1])
+        gates = keep.tile([P, SLOTS], F32, name="gates")
+        nc.sync.dma_start(gates[:], gate[0:P, :])
+        w2s = load_planes("w2s", w2_scales.rearrange("e s q n -> (e s) q n"), E * HP, N, nc.vector)
         w2w = keep.tile([P, E * HP * 2 * N], U8, name="w2w", align_bytes=64)
         nc.sync.dma_start(w2w[:].bitcast(I32).rearrange("p (g w) -> p g w", g=E * HP),
                           w2_words.bitcast(I32).rearrange("e s p w -> p (e s) w"))
-        gates = keep.tile([P, SLOTS], F32, name="gates")
-        nc.sync.dma_start(gates[:], gate[0:P, :])
-        load_both("w3w1", 1, w3_words[1])
-        resid = []
-        for nb in range(NB):
-            tile = keep.tile([P, T], F32, name="resid%d" % nb)
-            nc.sync.dma_start(tile[:], xr[nb * P:(nb + 1) * P, :])
-            resid.append(tile)
+        resid = keep.tile([P, NB * T], F32, name="resid")
+        nc.sync.dma_start(resid[:].rearrange("p (b t) -> p b t", b=NB), xr.rearrange("(b p) t -> p b t", b=NB))
 
         ident = keep.tile([P, P], F32, name="ident")
         make_identity(nc, ident[:])
@@ -146,13 +143,13 @@ def tile_moe_res_glu_silu_kernel(tc, x_words, x_scales, xr, w1_words, w1_scales,
 
         def gated(units):
             for bank, unit in zip(product(0, units), units):
-                acts[unit] = ring.tile([P, PASS], F32, name="act", bufs=4)
+                acts[unit] = ring.tile([P, PASS], F32, name="act", bufs=8)
                 nc.scalar.activation(acts[unit][:].rearrange("j (u p d) -> j u p d", u=2, d=2),
                                      bank[:].rearrange("j (p u d) -> j u p d", u=2, d=2), SILU)
 
         def hidden(unit):
             bank = product(1, [unit])[0]
-            hid[unit] = ring.tile([P, PASS], BF16, name="h", bufs=4)
+            hid[unit] = ring.tile([P, PASS], BF16, name="h", bufs=8)
             nc.vector.tensor_tensor(hid[unit][:].rearrange("j (u p d) -> j u p d", u=2, d=2),
                                     bank[:].rearrange("j (p u d) -> j u p d", u=2, d=2),
                                     acts[unit][:].rearrange("j (u p d) -> j u p d", u=2, d=2), MULT)
@@ -164,34 +161,31 @@ def tile_moe_res_glu_silu_kernel(tc, x_words, x_scales, xr, w1_words, w1_scales,
                 pairs = hid[b, hf][:].bitcast(F32)
                 for u in range(2):
                     nc.tensor.transpose(bank[:, (i * 2 + u) * P:(i * 2 + u + 1) * P], pairs[:, u * P:(u + 1) * P], ident[:])
-            ht = ring.tile([P, n * 2 * P], F32, name="ht", align_bytes=64)
+            ht = ring.tile([P, n * 2 * P], F32, name="ht", bufs=5, align_bytes=64)
             nc.scalar.copy(ht[:].rearrange("p (s j u) -> p s j u", s=n, u=2),
                            bank[:].rearrange("p (s u j) -> p s j u", s=n, u=2))
-            words = ring.tile([P, n * P], U32, name="hcodes", align_bytes=64)
-            scales = ring.tile([P, n * P], U8, name="hscales", align_bytes=64)
+            words = ring.tile([P, n * P], U32, name="hcodes", bufs=5, align_bytes=64)
+            scales = ring.tile([P, n * P], U8, name="hscales", bufs=5, align_bytes=64)
             nc.vector.quantize_mx(out=words[:].bitcast(FP8X4), scales=scales[:], in_=ht[:].bitcast(BF16))
             for i, hf in enumerate(halves):
                 codes[b, hf] = words[:, i * P:(i + 1) * P]
                 planes[b, hf] = scales[:, i * P:(i + 1) * P]
 
-        def second_layer(b):
+        def second_layer(b, nb):
             e = b * P // C
-            bank = psum.tile([P, NB * P], F32, name="ybank")
-            for nb in range(NB):
-                for s in range(HP):
-                    g = e * HP + s
-                    nc.tensor.matmul_mx(
-                        out=bank[:, nb * P:(nb + 1) * P],
-                        lhsT=w2w[:, (g * N + nb * P) * 2:(g * N + (nb + 1) * P) * 2].bitcast(FP4X4),
-                        lhsT_scale=w2s[:, g * N + nb * P:g * N + (nb + 1) * P],
-                        rhs=codes[b, s].bitcast(FP8X4),
-                        rhs_scale=planes[b, s],
-                        start=(s == 0), stop=(s == HP - 1))
-            y = ring.tile([P, NB * P], F32, name="y")
+            bank = psum.tile([P, P], F32, name="ybank")
+            for s in range(HP):
+                g = e * HP + s
+                nc.tensor.matmul_mx(
+                    out=bank[:],
+                    lhsT=w2w[:, (g * N + nb * P) * 2:(g * N + (nb + 1) * P) * 2].bitcast(FP4X4),
+                    lhsT_scale=w2s[:, g * N + nb * P:g * N + (nb + 1) * P],
+                    rhs=codes[b, s].bitcast(FP8X4), rhs_scale=planes[b, s],
+                    start=(s == 0), stop=(s == HP - 1))
+            y = ring.tile([P, P], F32, name="y", bufs=8)
             nc.scalar.copy(y[:], bank[:])
             lst = offsets[:, b * P // 16:(b + 1) * P // 16]
-            for nb in range(NB):
-                nc.vector.tensor_tensor(spread[nb][:].indirect(lst), y[:, nb * P:(nb + 1) * P], gates[:, b * P:(b + 1) * P], MULT)
+            nc.vector.tensor_tensor(spread[nb][:].indirect(lst), y[:], gates[:, b * P:(b + 1) * P], MULT)
 
         gated([(0, 0), (0, 1), (1, 0), (1, 1)])
         hidden((0, 0))
@@ -199,25 +193,25 @@ def tile_moe_res_glu_silu_kernel(tc, x_words, x_scales, xr, w1_words, w1_scales,
         hidden((1, 0))
         turn(0, (0, 1))
         hidden((1, 1))
-        gated([(2, 0)])
-        second_layer(0)
-        turn(1, (0, 1))
-        gated([(2, 1)])
-        hidden((2, 0))
-        hidden((2, 1))
-        second_layer(1)
-        gated([(3, 0)])
-        gated([(3, 1)])
-        turn(2, (0, 1))
-        hidden((3, 0))
-        hidden((3, 1))
+        for b in (2, 3):
+            gated([(b, 0)])
+            hidden((b, 0))
+            second_layer(b - 2, 0)
+            if b == 3:
+                turn(b - 1, (0, 1))
+            gated([(b, 1)])
+            hidden((b, 1))
+            if b == 2:
+                turn(b - 1, (0, 1))
+            second_layer(b - 2, 1)
         turn(3, (0,))
-        second_layer(2)
+        second_layer(2, 0)
         turn(3, (1,))
-        second_layer(3)
+        second_layer(2, 1)
+        second_layer(3, 0)
+        second_layer(3, 1)
 
-        for nb in range(NB):
-            for c0 in range(0, T, PASS):
-                res = ring.tile([P, PASS], F32, name="res", bufs=4)
-                nc.vector.tensor_tensor(res[:], spread[nb][:, c0:c0 + PASS], resid[nb][:, c0:c0 + PASS], ADD)
-                nc.sync.dma_start(out[nb * P:(nb + 1) * P, c0:c0 + PASS], res[:])
+        for nb, c0, c1 in ((0, 0, 512), (0, 512, 1024), (1, 0, 512), (1, 512, 768), (1, 768, 1024)):
+            res = ring.tile([P, c1 - c0], F32, name="res", bufs=5)
+            nc.vector.tensor_tensor(res[:], spread[nb][:, c0:c1], resid[:, nb * T + c0:nb * T + c1], ADD)
+            nc.sync.dma_start(out[nb * P:(nb + 1) * P, c0:c1], res[:])

@@ -57,7 +57,7 @@ def tile_moe_res_glu_silu_kernel(tc, x_words, x_scales, xr, w1_words, w1_scales,
             return tile
 
         zero = keep.tile([P, 2], F32, name="zero")
-        nc.vector.memset(zero[:, 0:1], 0.0)
+        nc.gpsimd.memset(zero[:, 0:1], 0.0)
         nc.scalar.activation(zero[:, 1:2], zero[:, 0:1], SILU)
 
         def load_half(name, words_hbm, hf):
@@ -69,12 +69,12 @@ def tile_moe_res_glu_silu_kernel(tc, x_words, x_scales, xr, w1_words, w1_scales,
         xw = {}
         wv = {}
         ws = {}
-        xs = load_planes("xs", x_scales, KP, T, nc.gpsimd)
         xw[0] = load_tokens(0)
+        xs = load_planes("xs", x_scales, KP, T, nc.vector)
         t = load_words("w1w00", w1_words[0, 0])
         for hf in range(HP):
             wv[0, 0, 0, hf] = t[:, hf * 2 * PASS:(hf + 1) * 2 * PASS]
-        ws[0] = load_planes("w1s", w1_scales.rearrange("e s q i -> (e s) q i"), E * KP, H, nc.gpsimd)
+        ws[0] = load_planes("w1s", w1_scales.rearrange("e s q i -> (e s) q i"), E * KP, H, nc.vector)
         xw[1] = load_tokens(1)
         t = load_words("w1w01", w1_words[0, 1])
         for hf in range(HP):
@@ -116,11 +116,12 @@ def tile_moe_res_glu_silu_kernel(tc, x_words, x_scales, xr, w1_words, w1_scales,
 
         gw = [keep.tile([P, SLOTS], U32, name="gw%d" % o, align_bytes=64) for o in range(KP)]
         gs = [keep.tile([P, SLOTS], U8, name="gs%d" % o, align_bytes=64) for o in range(KP)]
-        for o in range(KP):
-            for lo, hi in ((0, P), (P, C), (C, SLOTS)):
-                lst = offsets[:, lo // 16:hi // 16]
-                nc.vector.tensor_copy(gw[o][:, lo:hi], xw[o][:].bitcast(U32).indirect(lst))
-                nc.vector.tensor_copy(gs[o][:, lo:hi], xs[:, o * T:(o + 1) * T].indirect(lst))
+        for pieces in (((0, P), (P, C)), ((C, SLOTS),)):
+            for o in range(KP):
+                for lo, hi in pieces:
+                    lst = offsets[:, lo // 16:hi // 16]
+                    nc.vector.tensor_copy(gw[o][:, lo:hi], xw[o][:].bitcast(U32).indirect(lst))
+                    nc.vector.tensor_copy(gs[o][:, lo:hi], xs[:, o * T:(o + 1) * T].indirect(lst))
 
         acts = {}
         hid = {}
@@ -211,7 +212,7 @@ def tile_moe_res_glu_silu_kernel(tc, x_words, x_scales, xr, w1_words, w1_scales,
         second_layer(3, 0)
         second_layer(3, 1)
 
-        for nb, c0, c1 in ((0, 0, 512), (0, 512, 1024), (1, 0, 512), (1, 512, 768), (1, 768, 1024)):
+        for nb, c0, c1 in ((0, 0, 512), (0, 512, 1024), (1, 0, 512), (1, 512, 1024)):
             res = ring.tile([P, c1 - c0], F32, name="res", bufs=5)
             nc.vector.tensor_tensor(res[:], spread[nb][:, c0:c1], resid[:, nb * T + c0:nb * T + c1], ADD)
             nc.sync.dma_start(out[nb * P:(nb + 1) * P, c0:c1], res[:])

@@ -145,15 +145,12 @@ def tile_moe_res_glu_silu_kernel(tc, x_words, x_scales, xr, w1_words, w1_scales,
         def gated(units):
             for bank, unit in zip(product(0, units), units):
                 acts[unit] = ring.tile([P, PASS], F32, name="act", bufs=8)
-                nc.scalar.activation(acts[unit][:].rearrange("j (u p d) -> j u p d", u=2, d=2),
-                                     bank[:].rearrange("j (p u d) -> j u p d", u=2, d=2), SILU)
+                nc.scalar.activation(acts[unit][:], bank[:], SILU)
 
         def hidden(unit):
             bank = product(1, [unit])[0]
             hid[unit] = ring.tile([P, PASS], BF16, name="h", bufs=8)
-            nc.vector.tensor_tensor(hid[unit][:].rearrange("j (u p d) -> j u p d", u=2, d=2),
-                                    bank[:].rearrange("j (p u d) -> j u p d", u=2, d=2),
-                                    acts[unit][:].rearrange("j (u p d) -> j u p d", u=2, d=2), MULT)
+            nc.vector.tensor_tensor(hid[unit][:], bank[:], acts[unit][:], MULT)
 
         def turn(b, halves):
             n = len(halves)
@@ -161,7 +158,7 @@ def tile_moe_res_glu_silu_kernel(tc, x_words, x_scales, xr, w1_words, w1_scales,
             for i, hf in enumerate(halves):
                 pairs = hid[b, hf][:].bitcast(F32)
                 for u in range(2):
-                    nc.tensor.transpose(bank[:, (i * 2 + u) * P:(i * 2 + u + 1) * P], pairs[:, u * P:(u + 1) * P], ident[:])
+                    nc.tensor.transpose(bank[:, (i * 2 + u) * P:(i * 2 + u + 1) * P], pairs[:, u:2 * P:2], ident[:])
             ht = ring.tile([P, n * 2 * P], F32, name="ht", bufs=5, align_bytes=64)
             nc.scalar.copy(ht[:].rearrange("p (s j u) -> p s j u", s=n, u=2),
                            bank[:].rearrange("p (s u j) -> p s j u", s=n, u=2))

@@ -17,199 +17,208 @@ FP4X4 = mybir.dt.float4_e2m1fn_x4
 MULT = mybir.AluOpType.mult
 ADD = mybir.AluOpType.add
 SILU = mybir.ActivationFunctionType.Silu
+COPY = mybir.ActivationFunctionType.Copy
 
 P = 128
 PASS = 512
-KP = K // PASS
-HP = H // PASS
+K_PASSES = K // PASS
+H_PASSES = H // PASS
 SLOTS = E * C
 BLOCKS = SLOTS // P
-NB = N // P
+ROW_GROUPS = N // P
+FP4_BYTES = 2
+PER_COLUMN = 16
+W1, W3 = 0, 1
+FIRST_LAYER_BANKS = 6
 
 
-def tile_moe_res_glu_silu_kernel(tc, x_words, x_scales, xr, w1_words, w1_scales, w3_words, w3_scales, w2_words, w2_scales, gate, offs, out):
+def tile_moe_res_glu_silu_kernel(
+    tc, x_words, x_scales, xr, w1_words, w1_scales, w3_words, w3_scales, w2_words, w2_scales, gate, offs, out
+):
     nc = tc.nc
     with ExitStack() as ctx:
         keep = ctx.enter_context(tc.tile_pool(name="keep", bufs=1))
-        ring = ctx.enter_context(tc.tile_pool(name="ring", bufs=3))
+        work = ctx.enter_context(tc.tile_pool(name="work", bufs=1))
         psum = ctx.enter_context(tc.psum_pool(name="psum", bufs=1))
 
-        offsets = keep.tile([P, SLOTS // 16], U16, name="offsets")
+        offsets = keep.tile([P, SLOTS // PER_COLUMN], U16, name="offsets")
         nc.sync.dma_start(offsets[:], offs)
 
-        def load_planes(name, scales, planes, width, clearer):
-            tile = keep.tile([P, planes * width], U8, name=name, align_bytes=64)
-            words = tile[:].bitcast(I32)
-            clearer.memset(words, 0)
+        def slot_list(lo, hi):
+            return offsets[:, lo // PER_COLUMN:hi // PER_COLUMN]
+
+        def load_planes(name, scales, count, width):
+            tile = keep.tile([P, count * width], U8, name=name, align_bytes=64)
+            as_int = tile[:].bitcast(I32)
+            nc.vector.memset(as_int, 0)
             rows = scales.bitcast(I32).rearrange("g (q r) w -> r q g w", r=4)
             for r in range(4):
-                nc.sync.dma_start(words[r:P:32, :].rearrange("q (g w) -> q g w", g=planes), rows[r])
+                nc.sync.dma_start(as_int[r:P:32, :].rearrange("q (g w) -> q g w", g=count), rows[r])
             return tile
 
-        def load_words(name, words_hbm):
-            tile = keep.tile([P, words_hbm.shape[1]], U8, name=name, align_bytes=64)
-            nc.sync.dma_start(tile[:].bitcast(I32), words_hbm.bitcast(I32))
+        def load_passes(name, words):
+            count, width = words.shape[0], words.shape[2]
+            tile = keep.tile([P, count * width], U8, name=name, align_bytes=64)
+            nc.sync.dma_start(tile[:].bitcast(I32).rearrange("p (g w) -> p g w", g=count),
+                              words.bitcast(I32).rearrange("g p w -> p g w"))
             return tile
 
         def load_tokens(o):
-            tile = keep.tile([P, T], I32, name="xw%d" % o, align_bytes=64)
+            tile = keep.tile([P, T], I32, name="tokens%d" % o, align_bytes=64)
             nc.sync.dma_start(tile[:], x_words[o].rearrange("p t r -> p (t r)").bitcast(I32))
             return tile
 
-        zero = keep.tile([P, 2], F32, name="zero")
-        nc.gpsimd.memset(zero[:, 0:1], 0.0)
-        nc.scalar.activation(zero[:, 1:2], zero[:, 0:1], SILU)
+        seed = keep.tile([P, 2], F32, name="seed")
+        nc.gpsimd.memset(seed[:, 0:1], 0.0)
+        nc.scalar.activation(seed[:, 1:2], seed[:, 0:1], SILU)
 
-        def load_half(name, words_hbm, hf):
-            tile = keep.tile([P, KP * 2 * PASS], U8, name=name, align_bytes=64)
-            nc.sync.dma_start(tile[:].bitcast(I32).rearrange("p (s w) -> p s w", s=KP),
-                              words_hbm[:, :, hf * 2 * PASS:(hf + 1) * 2 * PASS].bitcast(I32).rearrange("s p w -> p s w"))
-            return tile
-
-        xw = {}
-        wv = {}
-        ws = {}
-        xw[0] = load_tokens(0)
-        xs = load_planes("xs", x_scales, KP, T, nc.vector)
-        t = load_words("w1w00", w1_words[0, 0])
-        for hf in range(HP):
-            wv[0, 0, 0, hf] = t[:, hf * 2 * PASS:(hf + 1) * 2 * PASS]
-        ws[0] = load_planes("w1s", w1_scales.rearrange("e s q i -> (e s) q i"), E * KP, H, nc.vector)
-        xw[1] = load_tokens(1)
-        t = load_words("w1w01", w1_words[0, 1])
-        for hf in range(HP):
-            wv[0, 0, 1, hf] = t[:, hf * 2 * PASS:(hf + 1) * 2 * PASS]
-        ws[1] = load_planes("w3s", w3_scales.rearrange("e s q i -> (e s) q i"), E * KP, H, nc.vector)
-        for hf in range(HP):
-            t = load_half("w3w0%d" % hf, w3_words[0], hf)
-            for o in range(KP):
-                wv[1, 0, o, hf] = t[:, o * 2 * PASS:(o + 1) * 2 * PASS]
-
-        def load_both(name, m, words_hbm):
-            tile = keep.tile([P, KP * 2 * H], U8, name=name, align_bytes=64)
-            nc.sync.dma_start(tile[:].bitcast(I32).rearrange("p (s w) -> p s w", s=KP),
-                              words_hbm.bitcast(I32).rearrange("s p w -> p s w"))
-            for o in range(KP):
-                for hf in range(HP):
-                    c0 = (o * H + hf * PASS) * 2
-                    wv[m, 1, o, hf] = tile[:, c0:c0 + 2 * PASS]
-
-        load_both("w1w1", 0, w1_words[1])
-        load_both("w3w1", 1, w3_words[1])
+        half_bytes = PASS * FP4_BYTES
+        tokens = {}
+        moving = {}
+        w_scales = {}
+        tokens[0] = load_tokens(0)
+        token_scales = load_planes("token_scales", x_scales, K_PASSES, T)
+        for o in range(K_PASSES):
+            if o > 0:
+                tokens[o] = load_tokens(o)
+            tile = load_passes("w1_e0_pass%d" % o, w1_words[0, o:o + 1])
+            for half in range(H_PASSES):
+                moving[W1, 0, o, half] = tile[:, half * half_bytes:(half + 1) * half_bytes]
+            if o == 0:
+                w_scales[W1] = load_planes("w1_scales", w1_scales.rearrange("e s q i -> (e s) q i"), E * K_PASSES, H)
+        w_scales[W3] = load_planes("w3_scales", w3_scales.rearrange("e s q i -> (e s) q i"), E * K_PASSES, H)
+        for half in range(H_PASSES):
+            tile = load_passes("w3_e0_half%d" % half, w3_words[0][:, :, half * half_bytes:(half + 1) * half_bytes])
+            for o in range(K_PASSES):
+                moving[W3, 0, o, half] = tile[:, o * half_bytes:(o + 1) * half_bytes]
+        for m, words in ((W1, w1_words), (W3, w3_words)):
+            tile = load_passes("w_e1_%d" % m, words[1])
+            for o in range(K_PASSES):
+                for half in range(H_PASSES):
+                    c0 = (o * H_PASSES + half) * half_bytes
+                    moving[m, 1, o, half] = tile[:, c0:c0 + half_bytes]
         gates = keep.tile([P, SLOTS], F32, name="gates")
         nc.sync.dma_start(gates[:], gate[0:P, :])
-        w2s = load_planes("w2s", w2_scales.rearrange("e s q n -> (e s) q n"), E * HP, N, nc.vector)
-        w2w = keep.tile([P, E * HP * 2 * N], U8, name="w2w", align_bytes=64)
-        nc.sync.dma_start(w2w[:].bitcast(I32).rearrange("p (g w) -> p g w", g=E * HP),
-                          w2_words.bitcast(I32).rearrange("e s p w -> p (e s) w"))
-        resid = keep.tile([P, NB * T], F32, name="resid")
-        nc.sync.dma_start(resid[:].rearrange("p (b t) -> p b t", b=NB), xr.rearrange("(b p) t -> p b t", b=NB))
+        w2_planes = load_planes("w2_scales", w2_scales.rearrange("e s q n -> (e s) q n"), E * H_PASSES, N)
+        w2_tile = load_passes("w2_words", w2_words.rearrange("e s p w -> (e s) p w"))
+        resid = keep.tile([P, ROW_GROUPS * T], F32, name="resid")
+        nc.sync.dma_start(resid[:].rearrange("p (g t) -> p g t", g=ROW_GROUPS), xr.rearrange("(g p) t -> p g t", g=ROW_GROUPS))
 
         ident = keep.tile([P, P], F32, name="ident")
         make_identity(nc, ident[:])
 
         spread = []
-        for nb in range(NB):
-            tile = keep.tile([P, T], F32, name="spread%d" % nb)
-            nc.scalar.copy(tile[:], zero[:, 0:1].to_broadcast([P, T]))
+        for g in range(ROW_GROUPS):
+            tile = keep.tile([P, T], F32, name="spread%d" % g)
+            nc.scalar.activation(tile[:], seed[:, 1:2].to_broadcast([P, T]), COPY, scale=0.0)
             spread.append(tile)
 
-        gw = [keep.tile([P, SLOTS], U32, name="gw%d" % o, align_bytes=64) for o in range(KP)]
-        gs = [keep.tile([P, SLOTS], U8, name="gs%d" % o, align_bytes=64) for o in range(KP)]
+        slot_words = [keep.tile([P, SLOTS], U32, name="slot_words%d" % o, align_bytes=64) for o in range(K_PASSES)]
+        slot_scales = [keep.tile([P, SLOTS], U8, name="slot_scales%d" % o, align_bytes=64) for o in range(K_PASSES)]
         for pieces in (((0, P), (P, C)), ((C, SLOTS),)):
-            for o in range(KP):
+            for o in range(K_PASSES):
                 for lo, hi in pieces:
-                    lst = offsets[:, lo // 16:hi // 16]
-                    nc.vector.tensor_copy(gw[o][:, lo:hi], xw[o][:].bitcast(U32).indirect(lst))
-                    nc.vector.tensor_copy(gs[o][:, lo:hi], xs[:, o * T:(o + 1) * T].indirect(lst))
+                    nc.vector.tensor_copy(slot_words[o][:, lo:hi], tokens[o][:].bitcast(U32).indirect(slot_list(lo, hi)))
+                    nc.vector.tensor_copy(slot_scales[o][:, lo:hi], token_scales[:, o * T:(o + 1) * T].indirect(slot_list(lo, hi)))
 
-        acts = {}
-        hid = {}
-        codes = {}
-        planes = {}
+        parts = BLOCKS * H_PASSES
+        silu_a = {}
+        hidden = {}
+        h_words = {}
+        h_scales = {}
 
-        def product(m, units):
-            banks = [psum.tile([P, PASS], F32, name="ab", bufs=6) for unit in units]
-            for o in range(KP):
-                for bank, (b, hf) in zip(banks, units):
+        def first_layer(m, some_parts):
+            banks = [psum.tile([P, PASS], F32, name="first", bufs=FIRST_LAYER_BANKS) for part in some_parts]
+            for o in range(K_PASSES):
+                for bank, (b, half) in zip(banks, some_parts):
                     e = b * P // C
-                    cols = slice(b * P, (b + 1) * P)
-                    s0 = (e * KP + o) * H + hf * PASS
+                    slots = slice(b * P, (b + 1) * P)
+                    c0 = (e * K_PASSES + o) * H + half * PASS
                     nc.tensor.matmul_mx(
                         out=bank[:],
-                        lhsT=gw[o][:, cols].bitcast(FP8X4), lhsT_scale=gs[o][:, cols],
-                        rhs=wv[m, e, o, hf].bitcast(FP4X4), rhs_scale=ws[m][:, s0:s0 + PASS],
-                        start=(o == 0), stop=(o == KP - 1))
+                        lhsT=slot_words[o][:, slots].bitcast(FP8X4), lhsT_scale=slot_scales[o][:, slots],
+                        rhs=moving[m, e, o, half].bitcast(FP4X4), rhs_scale=w_scales[m][:, c0:c0 + PASS],
+                        start=(o == 0), stop=(o == K_PASSES - 1))
             return banks
 
-        def gated(units):
-            for bank, unit in zip(product(0, units), units):
-                acts[unit] = ring.tile([P, PASS], F32, name="act", bufs=8)
-                nc.scalar.activation(acts[unit][:], bank[:], SILU)
+        def by_pairs(bank):
+            return bank[:].rearrange("j (p u d) -> j u p d", u=2, d=2)
 
-        def hidden(unit):
-            bank = product(1, [unit])[0]
-            hid[unit] = ring.tile([P, PASS], BF16, name="h", bufs=8)
-            nc.vector.tensor_tensor(hid[unit][:], bank[:], acts[unit][:], MULT)
+        def in_order(tile):
+            return tile[:].rearrange("j (u p d) -> j u p d", u=2, d=2)
 
-        def turn(b, halves):
+        def make_silu(some_parts):
+            for bank, part in zip(first_layer(W1, some_parts), some_parts):
+                silu_a[part] = work.tile([P, PASS], F32, name="silu_a", bufs=parts)
+                nc.scalar.activation(in_order(silu_a[part]), by_pairs(bank), SILU)
+
+        def make_hidden(part):
+            bank = first_layer(W3, [part])[0]
+            hidden[part] = work.tile([P, PASS], BF16, name="hidden", bufs=parts)
+            nc.vector.tensor_tensor(in_order(hidden[part]), by_pairs(bank), in_order(silu_a[part]), MULT)
+
+        def quantise(b, halves):
             n = len(halves)
             bank = psum.tile([P, n * 2 * P], F32, name="turned")
-            for i, hf in enumerate(halves):
-                pairs = hid[b, hf][:].bitcast(F32)
+            for s, half in enumerate(halves):
+                pairs = hidden[b, half][:].bitcast(F32)
                 for u in range(2):
-                    nc.tensor.transpose(bank[:, (i * 2 + u) * P:(i * 2 + u + 1) * P], pairs[:, u:2 * P:2], ident[:])
-            ht = ring.tile([P, n * 2 * P], F32, name="ht", bufs=5, align_bytes=64)
-            nc.scalar.copy(ht[:].rearrange("p (s j u) -> p s j u", s=n, u=2),
+                    nc.tensor.transpose(bank[:, (s * 2 + u) * P:(s * 2 + u + 1) * P], pairs[:, u * P:(u + 1) * P], ident[:])
+            turned = work.tile([P, n * 2 * P], F32, name="turned_sb", bufs=BLOCKS + 1, align_bytes=64)
+            nc.scalar.copy(turned[:].rearrange("p (s j u) -> p s j u", s=n, u=2),
                            bank[:].rearrange("p (s u j) -> p s j u", s=n, u=2))
-            words = ring.tile([P, n * P], U32, name="hcodes", bufs=5, align_bytes=64)
-            scales = ring.tile([P, n * P], U8, name="hscales", bufs=5, align_bytes=64)
-            nc.vector.quantize_mx(out=words[:].bitcast(FP8X4), scales=scales[:], in_=ht[:].bitcast(BF16))
-            for i, hf in enumerate(halves):
-                codes[b, hf] = words[:, i * P:(i + 1) * P]
-                planes[b, hf] = scales[:, i * P:(i + 1) * P]
+            words = work.tile([P, n * P], U32, name="h_words", bufs=BLOCKS + 1, align_bytes=64)
+            scales = work.tile([P, n * P], U8, name="h_scales", bufs=BLOCKS + 1, align_bytes=64)
+            nc.vector.quantize_mx(out=words[:].bitcast(FP8X4), scales=scales[:], in_=turned[:].bitcast(BF16))
+            for s, half in enumerate(halves):
+                h_words[b, half] = words[:, s * P:(s + 1) * P]
+                h_scales[b, half] = scales[:, s * P:(s + 1) * P]
 
-        def second_layer(b, nb):
+        def second_layer(b, groups):
             e = b * P // C
-            bank = psum.tile([P, P], F32, name="ybank")
-            for s in range(HP):
-                g = e * HP + s
-                nc.tensor.matmul_mx(
-                    out=bank[:],
-                    lhsT=w2w[:, (g * N + nb * P) * 2:(g * N + (nb + 1) * P) * 2].bitcast(FP4X4),
-                    lhsT_scale=w2s[:, g * N + nb * P:g * N + (nb + 1) * P],
-                    rhs=codes[b, s].bitcast(FP8X4), rhs_scale=planes[b, s],
-                    start=(s == 0), stop=(s == HP - 1))
-            y = ring.tile([P, P], F32, name="y", bufs=8)
+            bank = psum.tile([P, len(groups) * P], F32, name="second")
+            for s, g in enumerate(groups):
+                for half in range(H_PASSES):
+                    c0 = (e * H_PASSES + half) * N + g * P
+                    nc.tensor.matmul_mx(
+                        out=bank[:, s * P:(s + 1) * P],
+                        lhsT=w2_tile[:, c0 * FP4_BYTES:(c0 + P) * FP4_BYTES].bitcast(FP4X4),
+                        lhsT_scale=w2_planes[:, c0:c0 + P],
+                        rhs=h_words[b, half].bitcast(FP8X4), rhs_scale=h_scales[b, half],
+                        start=(half == 0), stop=(half == H_PASSES - 1))
+            y = work.tile([P, len(groups) * P], F32, name="y", bufs=BLOCKS * ROW_GROUPS)
             nc.scalar.copy(y[:], bank[:])
-            lst = offsets[:, b * P // 16:(b + 1) * P // 16]
-            nc.vector.tensor_tensor(spread[nb][:].indirect(lst), y[:], gates[:, b * P:(b + 1) * P], MULT)
+            for s, g in enumerate(groups):
+                nc.vector.tensor_tensor(spread[g][:].indirect(slot_list(b * P, (b + 1) * P)),
+                                        y[:, s * P:(s + 1) * P], gates[:, b * P:(b + 1) * P], MULT)
 
-        gated([(0, 0), (0, 1), (1, 0), (1, 1)])
-        hidden((0, 0))
-        hidden((0, 1))
-        hidden((1, 0))
-        turn(0, (0, 1))
-        hidden((1, 1))
-        for b in (2, 3):
-            gated([(b, 0)])
-            hidden((b, 0))
-            second_layer(b - 2, 0)
-            if b == 3:
-                turn(b - 1, (0, 1))
-            gated([(b, 1)])
-            hidden((b, 1))
-            if b == 2:
-                turn(b - 1, (0, 1))
-            second_layer(b - 2, 1)
-        turn(3, (0,))
-        second_layer(2, 0)
-        turn(3, (1,))
-        second_layer(2, 1)
-        second_layer(3, 0)
-        second_layer(3, 1)
+        make_silu([(0, 0), (0, 1), (1, 0), (1, 1)])
+        make_hidden((0, 0))
+        make_hidden((0, 1))
+        make_hidden((1, 0))
+        quantise(0, (0, 1))
+        make_hidden((1, 1))
+        make_silu([(2, 0)])
+        make_hidden((2, 0))
+        second_layer(0, (0,))
+        make_silu([(2, 1)])
+        make_hidden((2, 1))
+        quantise(1, (0, 1))
+        second_layer(0, (1,))
+        make_silu([(3, 0)])
+        make_hidden((3, 0))
+        second_layer(1, (0,))
+        quantise(2, (0, 1))
+        make_silu([(3, 1)])
+        make_hidden((3, 1))
+        second_layer(1, (1,))
+        quantise(3, (0,))
+        second_layer(2, (0, 1))
+        quantise(3, (1,))
+        second_layer(3, (0, 1))
 
-        for nb, c0, c1 in ((0, 0, 512), (0, 512, 1024), (1, 0, 512), (1, 512, 1024)):
-            res = ring.tile([P, c1 - c0], F32, name="res", bufs=5)
-            nc.vector.tensor_tensor(res[:], spread[nb][:, c0:c1], resid[:, nb * T + c0:nb * T + c1], ADD)
-            nc.sync.dma_start(out[nb * P:(nb + 1) * P, c0:c1], res[:])
+        for g in range(ROW_GROUPS):
+            for c0 in range(0, T, PASS):
+                total = work.tile([P, PASS], F32, name="total", bufs=ROW_GROUPS * T // PASS)
+                nc.vector.tensor_tensor(total[:], spread[g][:, c0:c0 + PASS], resid[:, g * T + c0:g * T + c0 + PASS], ADD)
+                nc.sync.dma_start(out[g * P:(g + 1) * P, c0:c0 + PASS], total[:])

from contextlib import ExitStack

import concourse.mybir as mybir
from concourse.masks import make_identity

K, T, E, C, H, N = 1024, 1024, 2, 256, 1024, 256
FLOPS = 2 * E * C * (2 * K * H + H * N)

F32 = mybir.dt.float32
BF16 = mybir.dt.bfloat16
I32 = mybir.dt.int32
U32 = mybir.dt.uint32
U16 = mybir.dt.uint16
U8 = mybir.dt.uint8
FP8X4 = mybir.dt.float8_e4m3fn_x4
FP4X4 = mybir.dt.float4_e2m1fn_x4
MULT = mybir.AluOpType.mult
ADD = mybir.AluOpType.add
SILU = mybir.ActivationFunctionType.Silu
COPY = mybir.ActivationFunctionType.Copy

P = 128
PASS = 512
K_PASSES = K // PASS
H_PASSES = H // PASS
SLOTS = E * C
BLOCKS = SLOTS // P
ROW_GROUPS = N // P
FP4_BYTES = 2
PER_COLUMN = 16
W1, W3 = 0, 1
FIRST_LAYER_BANKS = 6


def tile_moe_res_glu_silu_kernel(
    tc, x_words, x_scales, xr, w1_words, w1_scales, w3_words, w3_scales, w2_words, w2_scales, gate, offs, out
):
    nc = tc.nc
    with ExitStack() as ctx:
        keep = ctx.enter_context(tc.tile_pool(name="keep", bufs=1))
        work = ctx.enter_context(tc.tile_pool(name="work", bufs=1))
        psum = ctx.enter_context(tc.psum_pool(name="psum", bufs=1))

        offsets = keep.tile([P, SLOTS // PER_COLUMN], U16, name="offsets")
        nc.sync.dma_start(offsets[:], offs)

        def slot_list(lo, hi):
            return offsets[:, lo // PER_COLUMN:hi // PER_COLUMN]

        def load_planes(name, scales, count, width):
            tile = keep.tile([P, count * width], U8, name=name, align_bytes=64)
            as_int = tile[:].bitcast(I32)
            nc.vector.memset(as_int, 0)
            rows = scales.bitcast(I32).rearrange("g (q r) w -> r q g w", r=4)
            for r in range(4):
                nc.sync.dma_start(as_int[r:P:32, :].rearrange("q (g w) -> q g w", g=count), rows[r])
            return tile

        def load_passes(name, words):
            count, width = words.shape[0], words.shape[2]
            tile = keep.tile([P, count * width], U8, name=name, align_bytes=64)
            nc.sync.dma_start(tile[:].bitcast(I32).rearrange("p (g w) -> p g w", g=count),
                              words.bitcast(I32).rearrange("g p w -> p g w"))
            return tile

        def load_tokens(o):
            tile = keep.tile([P, T], I32, name="tokens%d" % o, align_bytes=64)
            nc.sync.dma_start(tile[:], x_words[o].rearrange("p t r -> p (t r)").bitcast(I32))
            return tile

        seed = keep.tile([P, 2], F32, name="seed")
        nc.gpsimd.memset(seed[:, 0:1], 0.0)
        nc.scalar.activation(seed[:, 1:2], seed[:, 0:1], SILU)

        half_bytes = PASS * FP4_BYTES
        tokens = {}
        moving = {}
        w_scales = {}
        tokens[0] = load_tokens(0)
        token_scales = load_planes("token_scales", x_scales, K_PASSES, T)
        for o in range(K_PASSES):
            if o > 0:
                tokens[o] = load_tokens(o)
            tile = load_passes("w1_e0_pass%d" % o, w1_words[0, o:o + 1])
            for half in range(H_PASSES):
                moving[W1, 0, o, half] = tile[:, half * half_bytes:(half + 1) * half_bytes]
            if o == 0:
                w_scales[W1] = load_planes("w1_scales", w1_scales.rearrange("e s q i -> (e s) q i"), E * K_PASSES, H)
        w_scales[W3] = load_planes("w3_scales", w3_scales.rearrange("e s q i -> (e s) q i"), E * K_PASSES, H)
        for half in range(H_PASSES):
            tile = load_passes("w3_e0_half%d" % half, w3_words[0][:, :, half * half_bytes:(half + 1) * half_bytes])
            for o in range(K_PASSES):
                moving[W3, 0, o, half] = tile[:, o * half_bytes:(o + 1) * half_bytes]
        for m, words in ((W1, w1_words), (W3, w3_words)):
            tile = load_passes("w_e1_%d" % m, words[1])
            for o in range(K_PASSES):
                for half in range(H_PASSES):
                    c0 = (o * H_PASSES + half) * half_bytes
                    moving[m, 1, o, half] = tile[:, c0:c0 + half_bytes]
        gates = keep.tile([P, SLOTS], F32, name="gates")
        nc.sync.dma_start(gates[:], gate[0:P, :])
        w2_planes = load_planes("w2_scales", w2_scales.rearrange("e s q n -> (e s) q n"), E * H_PASSES, N)
        w2_tile = load_passes("w2_words", w2_words.rearrange("e s p w -> (e s) p w"))
        resid = keep.tile([P, ROW_GROUPS * T], F32, name="resid")
        nc.sync.dma_start(resid[:].rearrange("p (g t) -> p g t", g=ROW_GROUPS), xr.rearrange("(g p) t -> p g t", g=ROW_GROUPS))

        ident = keep.tile([P, P], F32, name="ident")
        make_identity(nc, ident[:])

        spread = []
        for g in range(ROW_GROUPS):
            tile = keep.tile([P, T], F32, name="spread%d" % g)
            nc.scalar.activation(tile[:], seed[:, 1:2].to_broadcast([P, T]), COPY, scale=0.0)
            spread.append(tile)

        slot_words = [keep.tile([P, SLOTS], U32, name="slot_words%d" % o, align_bytes=64) for o in range(K_PASSES)]
        slot_scales = [keep.tile([P, SLOTS], U8, name="slot_scales%d" % o, align_bytes=64) for o in range(K_PASSES)]
        for pieces in (((0, P), (P, C)), ((C, SLOTS),)):
            for o in range(K_PASSES):
                for lo, hi in pieces:
                    nc.vector.tensor_copy(slot_words[o][:, lo:hi], tokens[o][:].bitcast(U32).indirect(slot_list(lo, hi)))
                    nc.vector.tensor_copy(slot_scales[o][:, lo:hi], token_scales[:, o * T:(o + 1) * T].indirect(slot_list(lo, hi)))

        parts = BLOCKS * H_PASSES
        silu_a = {}
        hidden = {}
        h_words = {}
        h_scales = {}

        def first_layer(m, some_parts):
            banks = [psum.tile([P, PASS], F32, name="first", bufs=FIRST_LAYER_BANKS) for part in some_parts]
            for o in range(K_PASSES):
                for bank, (b, half) in zip(banks, some_parts):
                    e = b * P // C
                    slots = slice(b * P, (b + 1) * P)
                    c0 = (e * K_PASSES + o) * H + half * PASS
                    nc.tensor.matmul_mx(
                        out=bank[:],
                        lhsT=slot_words[o][:, slots].bitcast(FP8X4), lhsT_scale=slot_scales[o][:, slots],
                        rhs=moving[m, e, o, half].bitcast(FP4X4), rhs_scale=w_scales[m][:, c0:c0 + PASS],
                        start=(o == 0), stop=(o == K_PASSES - 1))
            return banks

        def by_pairs(bank):
            return bank[:].rearrange("j (p u d) -> j u p d", u=2, d=2)

        def in_order(tile):
            return tile[:].rearrange("j (u p d) -> j u p d", u=2, d=2)

        def make_silu(some_parts):
            for bank, part in zip(first_layer(W1, some_parts), some_parts):
                silu_a[part] = work.tile([P, PASS], F32, name="silu_a", bufs=parts)
                nc.scalar.activation(in_order(silu_a[part]), by_pairs(bank), SILU)

        def make_hidden(part):
            bank = first_layer(W3, [part])[0]
            hidden[part] = work.tile([P, PASS], BF16, name="hidden", bufs=parts)
            nc.vector.tensor_tensor(in_order(hidden[part]), by_pairs(bank), in_order(silu_a[part]), MULT)

        def quantise(b, halves):
            n = len(halves)
            bank = psum.tile([P, n * 2 * P], F32, name="turned")
            for s, half in enumerate(halves):
                pairs = hidden[b, half][:].bitcast(F32)
                for u in range(2):
                    nc.tensor.transpose(bank[:, (s * 2 + u) * P:(s * 2 + u + 1) * P], pairs[:, u * P:(u + 1) * P], ident[:])
            turned = work.tile([P, n * 2 * P], F32, name="turned_sb", bufs=BLOCKS + 1, align_bytes=64)
            nc.scalar.copy(turned[:].rearrange("p (s j u) -> p s j u", s=n, u=2),
                           bank[:].rearrange("p (s u j) -> p s j u", s=n, u=2))
            words = work.tile([P, n * P], U32, name="h_words", bufs=BLOCKS + 1, align_bytes=64)
            scales = work.tile([P, n * P], U8, name="h_scales", bufs=BLOCKS + 1, align_bytes=64)
            nc.vector.quantize_mx(out=words[:].bitcast(FP8X4), scales=scales[:], in_=turned[:].bitcast(BF16))
            for s, half in enumerate(halves):
                h_words[b, half] = words[:, s * P:(s + 1) * P]
                h_scales[b, half] = scales[:, s * P:(s + 1) * P]

        def second_layer(b, groups):
            e = b * P // C
            bank = psum.tile([P, len(groups) * P], F32, name="second")
            for s, g in enumerate(groups):
                for half in range(H_PASSES):
                    c0 = (e * H_PASSES + half) * N + g * P
                    nc.tensor.matmul_mx(
                        out=bank[:, s * P:(s + 1) * P],
                        lhsT=w2_tile[:, c0 * FP4_BYTES:(c0 + P) * FP4_BYTES].bitcast(FP4X4),
                        lhsT_scale=w2_planes[:, c0:c0 + P],
                        rhs=h_words[b, half].bitcast(FP8X4), rhs_scale=h_scales[b, half],
                        start=(half == 0), stop=(half == H_PASSES - 1))
            y = work.tile([P, len(groups) * P], F32, name="y", bufs=BLOCKS * ROW_GROUPS)
            nc.scalar.copy(y[:], bank[:])
            for s, g in enumerate(groups):
                nc.vector.tensor_tensor(spread[g][:].indirect(slot_list(b * P, (b + 1) * P)),
                                        y[:, s * P:(s + 1) * P], gates[:, b * P:(b + 1) * P], MULT)

        make_silu([(0, 0), (0, 1), (1, 0), (1, 1)])
        make_hidden((0, 0))
        make_hidden((0, 1))
        make_hidden((1, 0))
        quantise(0, (0, 1))
        make_hidden((1, 1))
        make_silu([(2, 0)])
        make_hidden((2, 0))
        second_layer(0, (0,))
        make_silu([(2, 1)])
        make_hidden((2, 1))
        quantise(1, (0, 1))
        second_layer(0, (1,))
        make_silu([(3, 0)])
        make_hidden((3, 0))
        second_layer(1, (0,))
        quantise(2, (0, 1))
        make_silu([(3, 1)])
        make_hidden((3, 1))
        second_layer(1, (1,))
        quantise(3, (0,))
        second_layer(2, (0, 1))
        quantise(3, (1,))
        second_layer(3, (0, 1))

        for g in range(ROW_GROUPS):
            for c0 in range(0, T, PASS):
                total = work.tile([P, PASS], F32, name="total", bufs=ROW_GROUPS * T // PASS)
                nc.vector.tensor_tensor(total[:], spread[g][:, c0:c0 + PASS], resid[:, g * T + c0:g * T + c0 + PASS], ADD)
                nc.sync.dma_start(out[g * P:(g + 1) * P, c0:c0 + PASS], total[:])
